import numpy as np
import ml_dtypes


def mxq(x, axis, fmt="e4m3"):
    dtype, down = {"e4m3": (ml_dtypes.float8_e4m3fn, 7), "e5m2": (ml_dtypes.float8_e5m2, 14)}[fmt]
    v = np.moveaxis(np.asarray(x, np.float32).astype(ml_dtypes.bfloat16).astype(np.float64), axis, -1)
    blocks = v.reshape(v.shape[:-1] + (-1, 32))
    amax = np.abs(blocks).max(-1, keepdims=True)
    byte = np.maximum(np.where(amax > 0, np.frexp(amax)[1] - 1 + 127, 0) - down, 1)
    scale = np.exp2(byte - 127.0)
    codes = (blocks / scale).astype(np.float32).astype(dtype).astype(np.float64)
    return np.moveaxis((codes * scale).reshape(v.shape), -1, axis)


WIDE = False


def mx_kscale(k):
    if not WIDE:
        return np.ones(k)
    levels = np.array([10, -10, 5, -5, 0])
    if k % 512:
        return np.exp2(np.random.permutation(np.resize(levels, k // 32))).repeat(32)
    a = np.empty((k // 512, 16))
    for p in range(k // 512):
        a[p, :8] = np.random.permutation(np.resize(levels, 8))
        for g in range(8):
            far = levels[np.abs(levels - a[p, g]) >= 10]
            a[p, g + 8] = far[np.random.randint(len(far))]
    return np.exp2(a.ravel()).repeat(32)


def f64(x):
    return np.asarray(x).astype(np.float64)


def striped(idx):
    return np.tile(idx.reshape(-1, 16).T, (8, 1)).astype(np.uint16)


def unstriped(offs):
    return offs[:16].T.reshape(-1).astype(np.int64)


def relu(v):
    return np.maximum(v, 0.0)


K, T, E, C, H, N = 1024, 2048, 2, 256, 512, 512


def by_expert(wq, xq):
    return np.concatenate([wq[e].T @ xq[:, e * C:(e + 1) * C] for e in range(E)], axis=1)


def setup_inputs():
    n = np.random.standard_normal
    s = mx_kscale(K)[:, None]
    u = mx_kscale(H)
    return {
        "xT": (n((K, T)) * s).astype(np.float32),
        "w1": (n((E, K, H)) / np.sqrt(K) / s[None] * u[None, None, :]).astype(np.float32),
        "w2": (n((E, H, N)) / np.sqrt(H) / u[None, :, None]).astype(np.float32),
        "gate": np.tile(np.random.uniform(0.2, 1.0, E * C), (N, 1)).astype(np.float32),
        "offs": striped(np.random.permutation(T)[:E * C]),
    }


def reference(xT, w1, w2, gate, offs):
    idx = unstriped(offs)
    xq = mxq(f64(xT)[:, idx], 0, "e4m3")
    h = relu(by_expert(mxq(f64(w1), 1, "e4m3"), xq))
    y = by_expert(mxq(f64(w2), 1, "e4m3"), mxq(h, 0, "e4m3"))
    out = np.zeros((N, T))
    out[:, idx] = f64(gate) * y
    return out

@@ -1,0 +1,197 @@
+from contextlib import ExitStack
+
+import concourse.mybir as mybir
+
+K, T, E, C, H, N = 1024, 2048, 2, 256, 512, 512
+FLOPS = 2 * E * C * (K * H + H * N)
+
+F32 = mybir.dt.float32
+BF16 = mybir.dt.bfloat16
+U32 = mybir.dt.uint32
+U16 = mybir.dt.uint16
+U8 = mybir.dt.uint8
+FP8X4 = mybir.dt.float8_e4m3fn_x4
+MULT = mybir.AluOpType.mult
+RELU = mybir.ActivationFunctionType.Relu
+
+P = 128
+PACK = 4
+K_PASS = P * PACK
+G = K // K_PASS
+S = E * C
+HALF = 128
+NB = N // P
+LC = C // 16
+
+
+def tile_routed_moe_kernel(tc, xT, w1, w2, gate, offs, out):
+    nc = tc.nc
+    with ExitStack() as ctx:
+        held = ctx.enter_context(tc.tile_pool(name="held", bufs=1))
+        psum = ctx.enter_context(tc.psum_pool(name="psum", bufs=1))
+
+        offsets = held.tile([P, S // 16], U16, name="offsets")
+        nc.sync.dma_start(offsets[:], offs)
+
+        w1_raw = [[held.tile([P, PACK, H], F32, name="w1raw%d_%d" % (e, g)) for g in range(G)] for e in range(E)]
+        w2_raw = [[held.tile([P, PACK, N // 2], F32, name="w2raw%d_%d" % (e, q)) for q in range(2)] for e in range(E)]
+        planes = [[held.tile([P, T], F32, name="plane%d_%d" % (g, t)) for t in range(PACK)] for g in range(G)]
+        gate_sb = held.tile([P, S], F32, name="gate_sb")
+        x_view = xT.rearrange("(g p t) n -> g p t n", p=P, t=PACK)
+
+        def load_w1(e, g):
+            nc.sync.dma_start(
+                out=w1_raw[e][g][:],
+                in_=w1[e, g * K_PASS:(g + 1) * K_PASS, :].rearrange("(p j) c -> p j c", j=PACK),
+            )
+
+        def load_w2(e, q):
+            nc.sync.dma_start(
+                out=w2_raw[e][q][:],
+                in_=w2[e, :, q * (N // 2):(q + 1) * (N // 2)].rearrange("(p j) c -> p j c", j=PACK),
+            )
+
+        load_w1(0, 0)
+        for g in range(G):
+            for t in range(PACK):
+                nc.sync.dma_start(out=planes[g][t][:], in_=x_view[g, :, t, :])
+        load_w1(0, 1)
+        load_w1(1, 0)
+        load_w1(1, 1)
+        load_w2(0, 0)
+        nc.sync.dma_start(out=gate_sb[:], in_=gate[0:P, :])
+        load_w2(0, 1)
+        load_w2(1, 0)
+        load_w2(1, 1)
+
+        windows = [held.tile([P, T], F32, name="window%d" % nb) for nb in range(NB)]
+        for nb in range(NB):
+            nc.gpsimd.memset(windows[nb][:], 0.0)
+
+        w1_codes = [[held.tile([P, H], U32, name="w1_codes%d_%d" % (e, g), align_bytes=64) for g in range(G)] for e in range(E)]
+        w1_scales = [[held.tile([P, H], U8, name="w1_scales%d_%d" % (e, g), align_bytes=64) for g in range(G)] for e in range(E)]
+        w2_codes = [[held.tile([P, N // 2], U32, name="w2_codes%d_%d" % (e, q), align_bytes=64) for q in range(2)] for e in range(E)]
+        w2_scales = [[held.tile([P, N // 2], U8, name="w2_scales%d_%d" % (e, q), align_bytes=64) for q in range(2)] for e in range(E)]
+
+        def prep_w1(e, g, vt):
+            grouped = held.tile([P, PACK * H], BF16, name="w1_grouped%d_%d" % (e, g), align_bytes=64)
+            dst = grouped[:].rearrange("p (t m j) -> p m j t", t=PACK, j=PACK)
+            src = w1_raw[e][g][:].rearrange("p j (m t) -> p m j t", t=PACK)
+            vm = vt * P // PACK
+            if vm > 0:
+                nc.vector.tensor_copy(out=dst[:, 0:vm], in_=src[:, 0:vm])
+            if vm < P:
+                nc.scalar.copy(out=dst[:, vm:P], in_=src[:, vm:P])
+            nc.vector.quantize_mx(out=w1_codes[e][g][:].bitcast(FP8X4), scales=w1_scales[e][g][:], in_=grouped[:])
+
+        def prep_w2(e, q, engine, tag):
+            grouped = held.tile([P, N // 2, PACK], BF16, name="w2_grouped%d_%d" % (e, q), tag=tag, align_bytes=64)
+            src = w2_raw[e][q][:].rearrange("p j (c i) -> p c j i", i=PACK)
+            dst = grouped[:].rearrange("p (c i) j -> p c j i", i=PACK)
+            if engine == "v":
+                nc.vector.tensor_copy(out=dst, in_=src)
+            else:
+                nc.scalar.copy(out=dst, in_=src)
+            nc.vector.quantize_mx(
+                out=w2_codes[e][q][:].bitcast(FP8X4), scales=w2_scales[e][q][:], in_=grouped[:].rearrange("p n j -> p (n j)")
+            )
+
+        prep_w1(0, 0, 2)
+        prep_w1(0, 1, 2)
+
+        x_codes = [held.tile([P, S], U32, name="x_codes%d" % g, align_bytes=64) for g in range(G)]
+        x_scales = [held.tile([P, S], U8, name="x_scales%d" % g, align_bytes=64) for g in range(G)]
+        x_grouped = [held.tile([P, S, PACK], BF16, name="x_grouped%d" % g, align_bytes=64) for g in range(G)]
+
+        picked = held.tile([P, PACK, S], F32, name="picked")
+        for t in range(PACK):
+            nc.vector.tensor_copy(picked[:, t, :], planes[0][t][:].indirect(offsets[:]))
+        nc.scalar.copy(
+            out=x_grouped[0][:].rearrange("p (c i) t -> p c t i", i=PACK),
+            in_=picked[:].rearrange("p t (c i) -> p c t i", i=PACK),
+        )
+        nc.vector.quantize_mx(
+            out=x_codes[0][:].bitcast(FP8X4), scales=x_scales[0][:], in_=x_grouped[0][:].rearrange("p n t -> p (n t)")
+        )
+        for t in range(PACK - 1):
+            nc.vector.tensor_copy(x_grouped[1][:, :, t], planes[1][t][:].indirect(offsets[:]))
+        for e in range(E):
+            cols = slice(e * C, (e + 1) * C)
+            nc.vector.tensor_copy(
+                x_grouped[1][:, cols, PACK - 1], planes[1][PACK - 1][:].indirect(offsets[:, e * LC:(e + 1) * LC])
+            )
+            nc.vector.quantize_mx(
+                out=x_codes[1][:, cols].bitcast(FP8X4),
+                scales=x_scales[1][:, cols],
+                in_=x_grouped[1][:, cols, :].rearrange("p n t -> p (n t)"),
+            )
+
+        def layer1(e, relu_engines):
+            h_grouped = held.tile([P, C, PACK], BF16, name="h_grouped%d" % e, align_bytes=64)
+            for s in range(C // HALF):
+                bank = psum.tile([P, PACK, HALF], F32, name="a_bank%d_%d" % (e, s))
+                cols = slice(e * C + s * HALF, e * C + (s + 1) * HALF)
+                for t in range(PACK):
+                    for g in range(G):
+                        nc.tensor.matmul_mx(
+                            out=bank[:, t, :],
+                            lhsT=w1_codes[e][g][:, t * P:(t + 1) * P].bitcast(FP8X4),
+                            lhsT_scale=w1_scales[e][g][:, t * P:(t + 1) * P],
+                            rhs=x_codes[g][:, cols].bitcast(FP8X4),
+                            rhs_scale=x_scales[g][:, cols],
+                            start=(g == 0),
+                            stop=(g == G - 1),
+                        )
+                h_dst = h_grouped[:, s * HALF:(s + 1) * HALF, :]
+                h_src = bank[:].rearrange("p t n -> p n t")
+                if relu_engines[s] == "s":
+                    nc.scalar.activation(h_dst, h_src, RELU)
+                else:
+                    nc.vector.tensor_scalar_max(h_dst, h_src, 0.0)
+            h_codes = held.tile([P, C], U32, name="h_codes%d" % e, align_bytes=64)
+            h_scales = held.tile([P, C], U8, name="h_scales%d" % e, align_bytes=64)
+            nc.vector.quantize_mx(
+                out=h_codes[:].bitcast(FP8X4), scales=h_scales[:], in_=h_grouped[:].rearrange("p n t -> p (n t)")
+            )
+            return h_codes, h_scales
+
+        y_banks = [[psum.tile([P, 2, C], F32, name="y_bank%d_%d" % (e, q)) for q in range(2)] for e in range(E)]
+
+        def layer2(e, nb, hq, tag):
+            q, i = nb // 2, nb % 2
+            nc.tensor.matmul_mx(
+                out=y_banks[e][q][:, i, :],
+                lhsT=w2_codes[e][q][:, i * P:(i + 1) * P].bitcast(FP8X4),
+                lhsT_scale=w2_scales[e][q][:, i * P:(i + 1) * P],
+                rhs=hq[0][:].bitcast(FP8X4),
+                rhs_scale=hq[1][:],
+                start=True,
+                stop=True,
+            )
+            y_sb = held.tile([P, C], F32, name="y_sb%d_%d" % (e, nb), tag=tag, align_bytes=64)
+            nc.scalar.copy(out=y_sb[:], in_=y_banks[e][q][:, i, :])
+            return y_sb
+
+        def scatter(e, nb, y_sb):
+            nc.vector.tensor_tensor(
+                windows[nb][:].indirect(offsets[:, e * LC:(e + 1) * LC]),
+                y_sb[:],
+                gate_sb[:, e * C:(e + 1) * C],
+                MULT,
+            )
+
+        prep_w2(0, 0, "s", "w2g_aA")
+        ha = layer1(0, "sv")
+        prep_w1(1, 0, 2)
+        prep_w1(1, 1, 2)
+        hb = layer1(1, "ss")
+        prep_w2(0, 1, "v", "w2g_aB")
+        for nb in range(2):
+            scatter(0, nb, layer2(0, nb, ha, "y_a%d" % nb))
+        prep_w2(1, 0, "s", "w2g_bA")
+        prep_w2(1, 1, "s", "slot2")
+        scatter(0, 2, layer2(0, 2, ha, "slot2"))
+        scatter(0, 3, layer2(0, 3, ha, "y_a3"))
+        for nb in range(NB):
+            scatter(1, nb, layer2(1, nb, hb, "y_b%d" % nb))
+            nc.sync.dma_start(out=out[nb * P:(nb + 1) * P, :], in_=windows[nb][:])

@@ -26,6 +26,11 @@ LC = C // 16
 
 def tile_routed_moe_kernel(tc, xT, w1, w2, gate, offs, out):
     nc = tc.nc
+    loads = [("w1", 0, 0)] + [("x", g, t) for g in range(2) for t in range(4)] + [
+        ("w1", 0, 1), ("w1", 1, 0), ("w1", 1, 1), ("w2", 0, 0), ("gate", 0, 0), ("w2", 0, 1), ("w2", 1, 0), ("w2", 1, 1)]
+    vector_quarters = [[2, 3], [2, 0]]
+    w2_engine = ["vs", "ss"]
+    relu_engine = ["sv", "ss"]
     with ExitStack() as ctx:
         held = ctx.enter_context(tc.tile_pool(name="held", bufs=1))
         psum = ctx.enter_context(tc.psum_pool(name="psum", bufs=1))
@@ -39,30 +44,21 @@ def tile_routed_moe_kernel(tc, xT, w1, w2, gate, offs, out):
         gate_sb = held.tile([P, S], F32, name="gate_sb")
         x_view = xT.rearrange("(g p t) n -> g p t n", p=P, t=PACK)
 
-        def load_w1(e, g):
-            nc.sync.dma_start(
-                out=w1_raw[e][g][:],
-                in_=w1[e, g * K_PASS:(g + 1) * K_PASS, :].rearrange("(p j) c -> p j c", j=PACK),
-            )
-
-        def load_w2(e, q):
-            nc.sync.dma_start(
-                out=w2_raw[e][q][:],
-                in_=w2[e, :, q * (N // 2):(q + 1) * (N // 2)].rearrange("(p j) c -> p j c", j=PACK),
-            )
-
-        load_w1(0, 0)
-        for g in range(G):
-            for t in range(PACK):
-                nc.sync.dma_start(out=planes[g][t][:], in_=x_view[g, :, t, :])
-        load_w1(0, 1)
-        load_w1(1, 0)
-        load_w1(1, 1)
-        load_w2(0, 0)
-        nc.sync.dma_start(out=gate_sb[:], in_=gate[0:P, :])
-        load_w2(0, 1)
-        load_w2(1, 0)
-        load_w2(1, 1)
+        for kind, a, b in loads:
+            if kind == "w1":
+                nc.sync.dma_start(
+                    out=w1_raw[a][b][:],
+                    in_=w1[a, b * K_PASS:(b + 1) * K_PASS, :].rearrange("(p j) c -> p j c", j=PACK),
+                )
+            elif kind == "w2":
+                nc.sync.dma_start(
+                    out=w2_raw[a][b][:],
+                    in_=w2[a, :, b * (N // 2):(b + 1) * (N // 2)].rearrange("(p j) c -> p j c", j=PACK),
+                )
+            elif kind == "x":
+                nc.sync.dma_start(out=planes[a][b][:], in_=x_view[a, :, b, :])
+            else:
+                nc.sync.dma_start(out=gate_sb[:], in_=gate[0:P, :])
 
         windows = [held.tile([P, T], F32, name="window%d" % nb) for nb in range(NB)]
         for nb in range(NB):
@@ -73,22 +69,22 @@ def tile_routed_moe_kernel(tc, xT, w1, w2, gate, offs, out):
         w2_codes = [[held.tile([P, N // 2], U32, name="w2_codes%d_%d" % (e, q), align_bytes=64) for q in range(2)] for e in range(E)]
         w2_scales = [[held.tile([P, N // 2], U8, name="w2_scales%d_%d" % (e, q), align_bytes=64) for q in range(2)] for e in range(E)]
 
-        def prep_w1(e, g, vt):
+        def prep_w1(e, g):
             grouped = held.tile([P, PACK * H], BF16, name="w1_grouped%d_%d" % (e, g), align_bytes=64)
             dst = grouped[:].rearrange("p (t m j) -> p m j t", t=PACK, j=PACK)
             src = w1_raw[e][g][:].rearrange("p j (m t) -> p m j t", t=PACK)
-            vm = vt * P // PACK
+            vm = vector_quarters[e][g] * P // PACK
             if vm > 0:
                 nc.vector.tensor_copy(out=dst[:, 0:vm], in_=src[:, 0:vm])
             if vm < P:
                 nc.scalar.copy(out=dst[:, vm:P], in_=src[:, vm:P])
             nc.vector.quantize_mx(out=w1_codes[e][g][:].bitcast(FP8X4), scales=w1_scales[e][g][:], in_=grouped[:])
 
-        def prep_w2(e, q, engine, tag):
-            grouped = held.tile([P, N // 2, PACK], BF16, name="w2_grouped%d_%d" % (e, q), tag=tag, align_bytes=64)
+        def prep_w2(e, q):
+            grouped = held.tile([P, N // 2, PACK], BF16, name="w2_grouped%d_%d" % (e, q), align_bytes=64)
             src = w2_raw[e][q][:].rearrange("p j (c i) -> p c j i", i=PACK)
             dst = grouped[:].rearrange("p (c i) j -> p c j i", i=PACK)
-            if engine == "v":
+            if w2_engine[e][q] == "v":
                 nc.vector.tensor_copy(out=dst, in_=src)
             else:
                 nc.scalar.copy(out=dst, in_=src)
@@ -96,8 +92,8 @@ def tile_routed_moe_kernel(tc, xT, w1, w2, gate, offs, out):
                 out=w2_codes[e][q][:].bitcast(FP8X4), scales=w2_scales[e][q][:], in_=grouped[:].rearrange("p n j -> p (n j)")
             )
 
-        prep_w1(0, 0, 2)
-        prep_w1(0, 1, 2)
+        prep_w1(0, 0)
+        prep_w1(0, 1)
 
         x_codes = [held.tile([P, S], U32, name="x_codes%d" % g, align_bytes=64) for g in range(G)]
         x_scales = [held.tile([P, S], U8, name="x_scales%d" % g, align_bytes=64) for g in range(G)]
@@ -126,10 +122,10 @@ def tile_routed_moe_kernel(tc, xT, w1, w2, gate, offs, out):
                 in_=x_grouped[1][:, cols, :].rearrange("p n t -> p (n t)"),
             )
 
-        def layer1(e, relu_engines):
+        def layer1(e):
             h_grouped = held.tile([P, C, PACK], BF16, name="h_grouped%d" % e, align_bytes=64)
             for s in range(C // HALF):
-                bank = psum.tile([P, PACK, HALF], F32, name="a_bank%d_%d" % (e, s))
+                bank = psum.tile([P, PACK, HALF], F32, name="a_bank%d_%d" % (e, s), tag="bank%d" % (2 * e + s))
                 cols = slice(e * C + s * HALF, e * C + (s + 1) * HALF)
                 for t in range(PACK):
                     for g in range(G):
@@ -144,7 +140,7 @@ def tile_routed_moe_kernel(tc, xT, w1, w2, gate, offs, out):
                         )
                 h_dst = h_grouped[:, s * HALF:(s + 1) * HALF, :]
                 h_src = bank[:].rearrange("p t n -> p n t")
-                if relu_engines[s] == "s":
+                if relu_engine[e][s] == "s":
                     nc.scalar.activation(h_dst, h_src, RELU)
                 else:
                     nc.vector.tensor_scalar_max(h_dst, h_src, 0.0)
@@ -155,12 +151,11 @@ def tile_routed_moe_kernel(tc, xT, w1, w2, gate, offs, out):
             )
             return h_codes, h_scales
 
-        y_banks = [[psum.tile([P, 2, C], F32, name="y_bank%d_%d" % (e, q)) for q in range(2)] for e in range(E)]
-
-        def layer2(e, nb, hq, tag):
+        def layer2_and_scatter(e, nb, hq, bank_tag):
             q, i = nb // 2, nb % 2
+            y_bank = psum.tile([P, C], F32, name="y_bank%d_%d" % (e, nb), tag=bank_tag)
             nc.tensor.matmul_mx(
-                out=y_banks[e][q][:, i, :],
+                out=y_bank[:],
                 lhsT=w2_codes[e][q][:, i * P:(i + 1) * P].bitcast(FP8X4),
                 lhsT_scale=w2_scales[e][q][:, i * P:(i + 1) * P],
                 rhs=hq[0][:].bitcast(FP8X4),
@@ -168,11 +163,8 @@ def tile_routed_moe_kernel(tc, xT, w1, w2, gate, offs, out):
                 start=True,
                 stop=True,
             )
-            y_sb = held.tile([P, C], F32, name="y_sb%d_%d" % (e, nb), tag=tag, align_bytes=64)
-            nc.scalar.copy(out=y_sb[:], in_=y_banks[e][q][:, i, :])
-            return y_sb
-
-        def scatter(e, nb, y_sb):
+            y_sb = held.tile([P, C], F32, name="y_sb%d_%d" % (e, nb), align_bytes=64)
+            nc.scalar.copy(out=y_sb[:], in_=y_bank[:])
             nc.vector.tensor_tensor(
                 windows[nb][:].indirect(offsets[:, e * LC:(e + 1) * LC]),
                 y_sb[:],
@@ -180,18 +172,17 @@ def tile_routed_moe_kernel(tc, xT, w1, w2, gate, offs, out):
                 MULT,
             )
 
-        prep_w2(0, 0, "s", "w2g_aA")
-        ha = layer1(0, "sv")
-        prep_w1(1, 0, 2)
-        prep_w1(1, 1, 2)
-        hb = layer1(1, "ss")
-        prep_w2(0, 1, "v", "w2g_aB")
-        for nb in range(2):
-            scatter(0, nb, layer2(0, nb, ha, "y_a%d" % nb))
-        prep_w2(1, 0, "s", "w2g_bA")
-        prep_w2(1, 1, "s", "slot2")
-        scatter(0, 2, layer2(0, 2, ha, "slot2"))
-        scatter(0, 3, layer2(0, 3, ha, "y_a3"))
+        prep_w2(0, 0)
+        h = [None, None]
+        h[0] = layer1(0)
+        prep_w1(1, 0)
+        prep_w1(1, 1)
+        h[1] = layer1(1)
+        prep_w2(0, 1)
+        prep_w2(1, 0)
+        prep_w2(1, 1)
+        for e, nb, bank_tag in [(0, 0, "bank4"), (0, 1, "bank5"), (0, 2, "bank6"), (1, 0, "bank0"), (1, 1, "bank1"), (1, 2, "bank4"),
+                                (0, 3, "bank4"), (1, 3, "bank7")]:
+            layer2_and_scatter(e, nb, h[e], bank_tag)
         for nb in range(NB):
-            scatter(1, nb, layer2(1, nb, hb, "y_b%d" % nb))
             nc.sync.dma_start(out=out[nb * P:(nb + 1) * P, :], in_=windows[nb][:])

@@ -27,10 +27,10 @@ LC = C // 16
 def tile_routed_moe_kernel(tc, xT, w1, w2, gate, offs, out):
     nc = tc.nc
     loads = [("w1", 0, 0)] + [("x", g, t) for g in range(2) for t in range(4)] + [
-        ("w1", 0, 1), ("w1", 1, 0), ("w1", 1, 1), ("w2", 0, 0), ("gate", 0, 0), ("w2", 0, 1), ("w2", 1, 0), ("w2", 1, 1)]
-    vector_quarters = [[2, 3], [2, 0]]
+        ("w1", 0, 1), ("w1", 1, 0), ("w2", 0, 0), ("w1", 1, 1), ("gate", 0, 0), ("w2", 0, 1), ("w2", 1, 0), ("w2", 1, 1)]
+    vector_quarters = [[2, 2], [2, 2]]
     w2_engine = ["vs", "ss"]
-    relu_engine = ["sv", "ss"]
+    relu_engine = ["ss", "ss"]
     with ExitStack() as ctx:
         held = ctx.enter_context(tc.tile_pool(name="held", bufs=1))
         psum = ctx.enter_context(tc.psum_pool(name="psum", bufs=1))
@@ -163,11 +163,14 @@ def tile_routed_moe_kernel(tc, xT, w1, w2, gate, offs, out):
                 start=True,
                 stop=True,
             )
-            y_sb = held.tile([P, C], F32, name="y_sb%d_%d" % (e, nb), align_bytes=64)
-            nc.scalar.copy(out=y_sb[:], in_=y_bank[:])
+            if (e, nb) in tied:
+                y_sb = tied[(e, nb)]
+            else:
+                y_sb = held.tile([P, C], F32, name="y_sb%d_%d" % (e, nb))[:]
+            nc.scalar.copy(out=y_sb, in_=y_bank[:])
             nc.vector.tensor_tensor(
                 windows[nb][:].indirect(offsets[:, e * LC:(e + 1) * LC]),
-                y_sb[:],
+                y_sb,
                 gate_sb[:, e * C:(e + 1) * C],
                 MULT,
             )
@@ -181,6 +184,8 @@ def tile_routed_moe_kernel(tc, xT, w1, w2, gate, offs, out):
         prep_w2(0, 1)
         prep_w2(1, 0)
         prep_w2(1, 1)
+        y_pair = held.tile([P, 2, C], F32, name="y_pair", tag="w1raw1_1")
+        tied = {(0, 0): y_pair[:, 0, :], (0, 1): y_pair[:, 1, :]}
         for e, nb, bank_tag in [(0, 0, "bank4"), (0, 1, "bank5"), (0, 2, "bank6"), (1, 0, "bank0"), (1, 1, "bank1"), (1, 2, "bank4"),
                                 (0, 3, "bank4"), (1, 3, "bank7")]:
             layer2_and_scatter(e, nb, h[e], bank_tag)

@@ -28,7 +28,7 @@ def tile_routed_moe_kernel(tc, xT, w1, w2, gate, offs, out):
     nc = tc.nc
     loads = [("w1", 0, 0)] + [("x", g, t) for g in range(2) for t in range(4)] + [
         ("w1", 0, 1), ("w1", 1, 0), ("w2", 0, 0), ("w1", 1, 1), ("gate", 0, 0), ("w2", 0, 1), ("w2", 1, 0), ("w2", 1, 1)]
-    vector_quarters = [[2, 2], [2, 2]]
+    vector_quarters = [[2, 2], [2, 3]]
     w2_engine = ["vs", "ss"]
     relu_engine = ["ss", "ss"]
     with ExitStack() as ctx:

from contextlib import ExitStack

import concourse.mybir as mybir

K, T, E, C, H, N = 1024, 2048, 2, 256, 512, 512
FLOPS = 2 * E * C * (K * H + H * N)

F32 = mybir.dt.float32
BF16 = mybir.dt.bfloat16
U32 = mybir.dt.uint32
U16 = mybir.dt.uint16
U8 = mybir.dt.uint8
FP8X4 = mybir.dt.float8_e4m3fn_x4
MULT = mybir.AluOpType.mult
RELU = mybir.ActivationFunctionType.Relu

P = 128
PACK = 4
K_PASS = P * PACK
G = K // K_PASS
S = E * C
HALF = 128
NB = N // P
LC = C // 16


def tile_routed_moe_kernel(tc, xT, w1, w2, gate, offs, out):
    nc = tc.nc
    loads = [("w1", 0, 0)] + [("x", g, t) for g in range(2) for t in range(4)] + [
        ("w1", 0, 1), ("w1", 1, 0), ("w2", 0, 0), ("w1", 1, 1), ("gate", 0, 0), ("w2", 0, 1), ("w2", 1, 0), ("w2", 1, 1)]
    vector_quarters = [[2, 2], [2, 3]]
    w2_engine = ["vs", "ss"]
    relu_engine = ["ss", "ss"]
    with ExitStack() as ctx:
        held = ctx.enter_context(tc.tile_pool(name="held", bufs=1))
        psum = ctx.enter_context(tc.psum_pool(name="psum", bufs=1))

        offsets = held.tile([P, S // 16], U16, name="offsets")
        nc.sync.dma_start(offsets[:], offs)

        w1_raw = [[held.tile([P, PACK, H], F32, name="w1raw%d_%d" % (e, g)) for g in range(G)] for e in range(E)]
        w2_raw = [[held.tile([P, PACK, N // 2], F32, name="w2raw%d_%d" % (e, q)) for q in range(2)] for e in range(E)]
        planes = [[held.tile([P, T], F32, name="plane%d_%d" % (g, t)) for t in range(PACK)] for g in range(G)]
        gate_sb = held.tile([P, S], F32, name="gate_sb")
        x_view = xT.rearrange("(g p t) n -> g p t n", p=P, t=PACK)

        for kind, a, b in loads:
            if kind == "w1":
                nc.sync.dma_start(
                    out=w1_raw[a][b][:],
                    in_=w1[a, b * K_PASS:(b + 1) * K_PASS, :].rearrange("(p j) c -> p j c", j=PACK),
                )
            elif kind == "w2":
                nc.sync.dma_start(
                    out=w2_raw[a][b][:],
                    in_=w2[a, :, b * (N // 2):(b + 1) * (N // 2)].rearrange("(p j) c -> p j c", j=PACK),
                )
            elif kind == "x":
                nc.sync.dma_start(out=planes[a][b][:], in_=x_view[a, :, b, :])
            else:
                nc.sync.dma_start(out=gate_sb[:], in_=gate[0:P, :])

        windows = [held.tile([P, T], F32, name="window%d" % nb) for nb in range(NB)]
        for nb in range(NB):
            nc.gpsimd.memset(windows[nb][:], 0.0)

        w1_codes = [[held.tile([P, H], U32, name="w1_codes%d_%d" % (e, g), align_bytes=64) for g in range(G)] for e in range(E)]
        w1_scales = [[held.tile([P, H], U8, name="w1_scales%d_%d" % (e, g), align_bytes=64) for g in range(G)] for e in range(E)]
        w2_codes = [[held.tile([P, N // 2], U32, name="w2_codes%d_%d" % (e, q), align_bytes=64) for q in range(2)] for e in range(E)]
        w2_scales = [[held.tile([P, N // 2], U8, name="w2_scales%d_%d" % (e, q), align_bytes=64) for q in range(2)] for e in range(E)]

        def prep_w1(e, g):
            grouped = held.tile([P, PACK * H], BF16, name="w1_grouped%d_%d" % (e, g), align_bytes=64)
            dst = grouped[:].rearrange("p (t m j) -> p m j t", t=PACK, j=PACK)
            src = w1_raw[e][g][:].rearrange("p j (m t) -> p m j t", t=PACK)
            vm = vector_quarters[e][g] * P // PACK
            if vm > 0:
                nc.vector.tensor_copy(out=dst[:, 0:vm], in_=src[:, 0:vm])
            if vm < P:
                nc.scalar.copy(out=dst[:, vm:P], in_=src[:, vm:P])
            nc.vector.quantize_mx(out=w1_codes[e][g][:].bitcast(FP8X4), scales=w1_scales[e][g][:], in_=grouped[:])

        def prep_w2(e, q):
            grouped = held.tile([P, N // 2, PACK], BF16, name="w2_grouped%d_%d" % (e, q), align_bytes=64)
            src = w2_raw[e][q][:].rearrange("p j (c i) -> p c j i", i=PACK)
            dst = grouped[:].rearrange("p (c i) j -> p c j i", i=PACK)
            if w2_engine[e][q] == "v":
                nc.vector.tensor_copy(out=dst, in_=src)
            else:
                nc.scalar.copy(out=dst, in_=src)
            nc.vector.quantize_mx(
                out=w2_codes[e][q][:].bitcast(FP8X4), scales=w2_scales[e][q][:], in_=grouped[:].rearrange("p n j -> p (n j)")
            )

        prep_w1(0, 0)
        prep_w1(0, 1)

        x_codes = [held.tile([P, S], U32, name="x_codes%d" % g, align_bytes=64) for g in range(G)]
        x_scales = [held.tile([P, S], U8, name="x_scales%d" % g, align_bytes=64) for g in range(G)]
        x_grouped = [held.tile([P, S, PACK], BF16, name="x_grouped%d" % g, align_bytes=64) for g in range(G)]

        picked = held.tile([P, PACK, S], F32, name="picked")
        for t in range(PACK):
            nc.vector.tensor_copy(picked[:, t, :], planes[0][t][:].indirect(offsets[:]))
        nc.scalar.copy(
            out=x_grouped[0][:].rearrange("p (c i) t -> p c t i", i=PACK),
            in_=picked[:].rearrange("p t (c i) -> p c t i", i=PACK),
        )
        nc.vector.quantize_mx(
            out=x_codes[0][:].bitcast(FP8X4), scales=x_scales[0][:], in_=x_grouped[0][:].rearrange("p n t -> p (n t)")
        )
        for t in range(PACK - 1):
            nc.vector.tensor_copy(x_grouped[1][:, :, t], planes[1][t][:].indirect(offsets[:]))
        for e in range(E):
            cols = slice(e * C, (e + 1) * C)
            nc.vector.tensor_copy(
                x_grouped[1][:, cols, PACK - 1], planes[1][PACK - 1][:].indirect(offsets[:, e * LC:(e + 1) * LC])
            )
            nc.vector.quantize_mx(
                out=x_codes[1][:, cols].bitcast(FP8X4),
                scales=x_scales[1][:, cols],
                in_=x_grouped[1][:, cols, :].rearrange("p n t -> p (n t)"),
            )

        def layer1(e):
            h_grouped = held.tile([P, C, PACK], BF16, name="h_grouped%d" % e, align_bytes=64)
            for s in range(C // HALF):
                bank = psum.tile([P, PACK, HALF], F32, name="a_bank%d_%d" % (e, s), tag="bank%d" % (2 * e + s))
                cols = slice(e * C + s * HALF, e * C + (s + 1) * HALF)
                for t in range(PACK):
                    for g in range(G):
                        nc.tensor.matmul_mx(
                            out=bank[:, t, :],
                            lhsT=w1_codes[e][g][:, t * P:(t + 1) * P].bitcast(FP8X4),
                            lhsT_scale=w1_scales[e][g][:, t * P:(t + 1) * P],
                            rhs=x_codes[g][:, cols].bitcast(FP8X4),
                            rhs_scale=x_scales[g][:, cols],
                            start=(g == 0),
                            stop=(g == G - 1),
                        )
                h_dst = h_grouped[:, s * HALF:(s + 1) * HALF, :]
                h_src = bank[:].rearrange("p t n -> p n t")
                if relu_engine[e][s] == "s":
                    nc.scalar.activation(h_dst, h_src, RELU)
                else:
                    nc.vector.tensor_scalar_max(h_dst, h_src, 0.0)
            h_codes = held.tile([P, C], U32, name="h_codes%d" % e, align_bytes=64)
            h_scales = held.tile([P, C], U8, name="h_scales%d" % e, align_bytes=64)
            nc.vector.quantize_mx(
                out=h_codes[:].bitcast(FP8X4), scales=h_scales[:], in_=h_grouped[:].rearrange("p n t -> p (n t)")
            )
            return h_codes, h_scales

        def layer2_and_scatter(e, nb, hq, bank_tag):
            q, i = nb // 2, nb % 2
            y_bank = psum.tile([P, C], F32, name="y_bank%d_%d" % (e, nb), tag=bank_tag)
            nc.tensor.matmul_mx(
                out=y_bank[:],
                lhsT=w2_codes[e][q][:, i * P:(i + 1) * P].bitcast(FP8X4),
                lhsT_scale=w2_scales[e][q][:, i * P:(i + 1) * P],
                rhs=hq[0][:].bitcast(FP8X4),
                rhs_scale=hq[1][:],
                start=True,
                stop=True,
            )
            if (e, nb) in tied:
                y_sb = tied[(e, nb)]
            else:
                y_sb = held.tile([P, C], F32, name="y_sb%d_%d" % (e, nb))[:]
            nc.scalar.copy(out=y_sb, in_=y_bank[:])
            nc.vector.tensor_tensor(
                windows[nb][:].indirect(offsets[:, e * LC:(e + 1) * LC]),
                y_sb,
                gate_sb[:, e * C:(e + 1) * C],
                MULT,
            )

        prep_w2(0, 0)
        h = [None, None]
        h[0] = layer1(0)
        prep_w1(1, 0)
        prep_w1(1, 1)
        h[1] = layer1(1)
        prep_w2(0, 1)
        prep_w2(1, 0)
        prep_w2(1, 1)
        y_pair = held.tile([P, 2, C], F32, name="y_pair", tag="w1raw1_1")
        tied = {(0, 0): y_pair[:, 0, :], (0, 1): y_pair[:, 1, :]}
        for e, nb, bank_tag in [(0, 0, "bank4"), (0, 1, "bank5"), (0, 2, "bank6"), (1, 0, "bank0"), (1, 1, "bank1"), (1, 2, "bank4"),
                                (0, 3, "bank4"), (1, 3, "bank7")]:
            layer2_and_scatter(e, nb, h[e], bank_tag)
        for nb in range(NB):
            nc.sync.dma_start(out=out[nb * P:(nb + 1) * P, :], in_=windows[nb][:])
